import numpy as np
import ml_dtypes

BF16 = ml_dtypes.bfloat16


def bf(x):
    return np.asarray(x, np.float32).astype(BF16)


def f32(x):
    return np.asarray(x, np.float32)


def f64(x):
    return np.asarray(x).astype(np.float64)


def striped(idx):
    return np.tile(idx.reshape(-1, 16).T, (8, 1))


S, K, M, N = 1024, 128, 128, 256


def setup_inputs():
    return {"table": bf(np.random.standard_normal((K, S))), "w": bf(np.random.standard_normal((K, M)) / np.sqrt(K)), "r": f32(np.random.standard_normal((M, N))), "s": f32(0.5 + np.random.random_sample((M, 1))), "offs": striped(np.random.permutation(np.tile(np.arange(S), 2))[:N])}


def reference(table, w, r, s, offs):
    idx = offs[:16].T.reshape(-1)
    z = f64(w).T @ f64(table)[:, idx] + f64(r)
    z = z / np.sqrt((z**2).mean(axis=0, keepdims=True) + 1e-5) * f64(s)
    return z

@@ -1,0 +1,58 @@
+import concourse.mybir as mybir
+
+F32, BF16, U16 = mybir.dt.float32, mybir.dt.bfloat16, mybir.dt.uint16
+ALU = mybir.AluOpType
+ACT = mybir.ActivationFunctionType
+
+S, K, M, N = 1024, 128, 128, 256
+EPS = 1e-5
+GROUP = 16
+PIECES = 2
+PIECE = N // PIECES
+
+FLOPS = 2 * K * M * N
+
+
+def tile_rows_embnorm_rep_kernel(tc, table, w, r, s, offs, out):
+    nc = tc.nc
+    with (
+        tc.tile_pool(name="held", bufs=1) as held,
+        tc.tile_pool(name="work", bufs=PIECES) as work,
+        tc.psum_pool(name="psum", bufs=PIECES) as psum,
+    ):
+        table_sb = held.tile([K, S], BF16)
+        w_sb = held.tile([K, M], BF16)
+        r_sb = held.tile([M, N], F32)
+        s_sb = held.tile([M, 1], F32)
+        offsets = held.tile([128, N // GROUP], U16)
+        nc.scalar.dma_start(table_sb[:], table)
+        nc.sync.dma_start(offsets[:], offs)
+        nc.sync.dma_start(w_sb[:], w)
+        nc.scalar.dma_start(r_sb[:], r)
+        nc.sync.dma_start(s_sb[:], s)
+
+        averager = held.tile([M, M], BF16)
+        eps = held.tile([M, 1], F32)
+        nc.vector.memset(averager[:], 1.0 / M)
+        nc.vector.memset(eps[:], EPS)
+
+        projected = []
+        for p in range(PIECES):
+            picked = table_sb[:].indirect(offsets[:, p * PIECE // GROUP : (p + 1) * PIECE // GROUP])
+            y = psum.tile([M, PIECE], F32)
+            nc.tensor.matmul(y[:], w_sb[:], picked, start=True, stop=True)
+            projected.append(y)
+
+        for p in range(PIECES):
+            cols = slice(p * PIECE, (p + 1) * PIECE)
+            z = work.tile([M, PIECE], F32)
+            nc.vector.tensor_tensor(z[:], projected[p][:], r_sb[:, cols], ALU.add)
+            squares = work.tile([M, PIECE], BF16)
+            nc.scalar.activation(squares[:], z[:], ACT.Square)
+            mean_square = psum.tile([M, PIECE], F32)
+            nc.tensor.matmul(mean_square[:], averager[:], squares[:], start=True, stop=True)
+            inv_rms = work.tile([M, PIECE], F32)
+            nc.scalar.activation(inv_rms[:], mean_square[:], ACT.Abs_reciprocal_sqrt, bias=eps[:])
+            normed = work.tile([M, PIECE], F32)
+            nc.vector.scalar_tensor_tensor(normed[:], z[:], s_sb[:], inv_rms[:], ALU.mult, ALU.mult)
+            nc.sync.dma_start(out[:, cols], normed[:])

@@ -35,6 +35,8 @@ def tile_rows_embnorm_rep_kernel(tc, table, w, r, s, offs, out):
         eps = held.tile([M, 1], F32)
         nc.vector.memset(averager[:], 1.0 / M)
         nc.vector.memset(eps[:], EPS)
+        warm = held.tile([M, 1], F32)
+        nc.scalar.activation(warm[:], eps[:], ACT.Abs_reciprocal_sqrt, bias=eps[:])
 
         projected = []
         for p in range(PIECES):

@@ -7,8 +7,10 @@ ACT = mybir.ActivationFunctionType
 S, K, M, N = 1024, 128, 128, 256
 EPS = 1e-5
 GROUP = 16
-PIECES = 2
-PIECE = N // PIECES
+WIDTHS = (64, 64, 64, 64,)
+PIECES = len(WIDTHS)
+STARTS = [sum(WIDTHS[:p]) for p in range(PIECES + 1)]
+PIECES_PER_STORE = 2
 
 FLOPS = 2 * K * M * N
 
@@ -31,6 +33,7 @@ def tile_rows_embnorm_rep_kernel(tc, table, w, r, s, offs, out):
         nc.scalar.dma_start(r_sb[:], r)
         nc.sync.dma_start(s_sb[:], s)
 
+        normed = held.tile([M, N], F32)
         averager = held.tile([M, M], BF16)
         eps = held.tile([M, 1], F32)
         nc.vector.memset(averager[:], 1.0 / M)
@@ -40,21 +43,22 @@ def tile_rows_embnorm_rep_kernel(tc, table, w, r, s, offs, out):
 
         projected = []
         for p in range(PIECES):
-            picked = table_sb[:].indirect(offsets[:, p * PIECE // GROUP : (p + 1) * PIECE // GROUP])
-            y = psum.tile([M, PIECE], F32)
+            picked = table_sb[:].indirect(offsets[:, STARTS[p] // GROUP : STARTS[p + 1] // GROUP])
+            y = psum.tile([M, WIDTHS[p]], F32)
             nc.tensor.matmul(y[:], w_sb[:], picked, start=True, stop=True)
             projected.append(y)
 
         for p in range(PIECES):
-            cols = slice(p * PIECE, (p + 1) * PIECE)
-            z = work.tile([M, PIECE], F32)
+            cols = slice(STARTS[p], STARTS[p + 1])
+            z = work.tile([M, WIDTHS[p]], F32)
             nc.vector.tensor_tensor(z[:], projected[p][:], r_sb[:, cols], ALU.add)
-            squares = work.tile([M, PIECE], BF16)
+            squares = work.tile([M, WIDTHS[p]], BF16)
             nc.scalar.activation(squares[:], z[:], ACT.Square)
-            mean_square = psum.tile([M, PIECE], F32)
+            mean_square = psum.tile([M, WIDTHS[p]], F32)
             nc.tensor.matmul(mean_square[:], averager[:], squares[:], start=True, stop=True)
-            inv_rms = work.tile([M, PIECE], F32)
+            inv_rms = work.tile([M, WIDTHS[p]], F32)
             nc.scalar.activation(inv_rms[:], mean_square[:], ACT.Abs_reciprocal_sqrt, bias=eps[:])
-            normed = work.tile([M, PIECE], F32)
-            nc.vector.scalar_tensor_tensor(normed[:], z[:], s_sb[:], inv_rms[:], ALU.mult, ALU.mult)
-            nc.sync.dma_start(out[:, cols], normed[:])
+            nc.vector.scalar_tensor_tensor(normed[:, cols], z[:], s_sb[:], inv_rms[:], ALU.mult, ALU.mult)
+            if (p + 1) % PIECES_PER_STORE == 0:
+                stored = slice(STARTS[p + 1 - PIECES_PER_STORE], STARTS[p + 1])
+                nc.sync.dma_start(out[:, stored], normed[:, stored])

@@ -27,10 +27,10 @@ def tile_rows_embnorm_rep_kernel(tc, table, w, r, s, offs, out):
         r_sb = held.tile([M, N], F32)
         s_sb = held.tile([M, 1], F32)
         offsets = held.tile([128, N // GROUP], U16)
-        nc.scalar.dma_start(table_sb[:], table)
+        nc.sync.dma_start(table_sb[:], table)
+        nc.scalar.dma_start(w_sb[:], w)
         nc.sync.dma_start(offsets[:], offs)
-        nc.sync.dma_start(w_sb[:], w)
-        nc.scalar.dma_start(r_sb[:], r)
+        nc.sync.dma_start(r_sb[:], r)
         nc.sync.dma_start(s_sb[:], s)
 
         normed = held.tile([M, N], F32)
@@ -53,7 +53,7 @@ def tile_rows_embnorm_rep_kernel(tc, table, w, r, s, offs, out):
             z = work.tile([M, WIDTHS[p]], F32)
             nc.vector.tensor_tensor(z[:], projected[p][:], r_sb[:, cols], ALU.add)
             squares = work.tile([M, WIDTHS[p]], BF16)
-            nc.scalar.activation(squares[:], z[:], ACT.Square)
+            nc.vector.tensor_tensor(squares[:], z[:], z[:], ALU.mult)
             mean_square = psum.tile([M, WIDTHS[p]], F32)
             nc.tensor.matmul(mean_square[:], averager[:], squares[:], start=True, stop=True)
             inv_rms = work.tile([M, WIDTHS[p]], F32)

import concourse.mybir as mybir

F32, BF16, U16 = mybir.dt.float32, mybir.dt.bfloat16, mybir.dt.uint16
ALU = mybir.AluOpType
ACT = mybir.ActivationFunctionType

S, K, M, N = 1024, 128, 128, 256
EPS = 1e-5
GROUP = 16
WIDTHS = (64, 64, 64, 64,)
PIECES = len(WIDTHS)
STARTS = [sum(WIDTHS[:p]) for p in range(PIECES + 1)]
PIECES_PER_STORE = 2

FLOPS = 2 * K * M * N


def tile_rows_embnorm_rep_kernel(tc, table, w, r, s, offs, out):
    nc = tc.nc
    with (
        tc.tile_pool(name="held", bufs=1) as held,
        tc.tile_pool(name="work", bufs=PIECES) as work,
        tc.psum_pool(name="psum", bufs=PIECES) as psum,
    ):
        table_sb = held.tile([K, S], BF16)
        w_sb = held.tile([K, M], BF16)
        r_sb = held.tile([M, N], F32)
        s_sb = held.tile([M, 1], F32)
        offsets = held.tile([128, N // GROUP], U16)
        nc.sync.dma_start(table_sb[:], table)
        nc.scalar.dma_start(w_sb[:], w)
        nc.sync.dma_start(offsets[:], offs)
        nc.sync.dma_start(r_sb[:], r)
        nc.sync.dma_start(s_sb[:], s)

        normed = held.tile([M, N], F32)
        averager = held.tile([M, M], BF16)
        eps = held.tile([M, 1], F32)
        nc.vector.memset(averager[:], 1.0 / M)
        nc.vector.memset(eps[:], EPS)
        warm = held.tile([M, 1], F32)
        nc.scalar.activation(warm[:], eps[:], ACT.Abs_reciprocal_sqrt, bias=eps[:])

        projected = []
        for p in range(PIECES):
            picked = table_sb[:].indirect(offsets[:, STARTS[p] // GROUP : STARTS[p + 1] // GROUP])
            y = psum.tile([M, WIDTHS[p]], F32)
            nc.tensor.matmul(y[:], w_sb[:], picked, start=True, stop=True)
            projected.append(y)

        for p in range(PIECES):
            cols = slice(STARTS[p], STARTS[p + 1])
            z = work.tile([M, WIDTHS[p]], F32)
            nc.vector.tensor_tensor(z[:], projected[p][:], r_sb[:, cols], ALU.add)
            squares = work.tile([M, WIDTHS[p]], BF16)
            nc.vector.tensor_tensor(squares[:], z[:], z[:], ALU.mult)
            mean_square = psum.tile([M, WIDTHS[p]], F32)
            nc.tensor.matmul(mean_square[:], averager[:], squares[:], start=True, stop=True)
            inv_rms = work.tile([M, WIDTHS[p]], F32)
            nc.scalar.activation(inv_rms[:], mean_square[:], ACT.Abs_reciprocal_sqrt, bias=eps[:])
            nc.vector.scalar_tensor_tensor(normed[:, cols], z[:], s_sb[:], inv_rms[:], ALU.mult, ALU.mult)
            if (p + 1) % PIECES_PER_STORE == 0:
                stored = slice(STARTS[p + 1 - PIECES_PER_STORE], STARTS[p + 1])
                nc.sync.dma_start(out[:, stored], normed[:, stored])
